import numpy as np
import ml_dtypes

BF16 = ml_dtypes.bfloat16


def bf(x):
    return np.asarray(x, np.float32).astype(BF16)


def f32(x):
    return np.asarray(x, np.float32)


def f64(x):
    return np.asarray(x).astype(np.float64)


def striped(idx):
    return np.tile(idx.reshape(-1, 16).T, (8, 1))


S, K, M, N, E, Q = 1024, 512, 128, 2048, 4, 512


def gelu_tanh(v):
    return 0.5 * v * (1.0 + np.tanh(np.sqrt(2.0 / np.pi) * (v + 0.044715 * v**3)))


def two_experts():
    first = np.random.permutation(S).reshape(E, S // E)
    return np.concatenate([np.random.permutation(np.concatenate([first[e], first[(e + 1) % E]])) for e in range(E)])


def setup_inputs():
    return {"table": bf(np.random.standard_normal((K, S))), "w": bf(np.random.standard_normal((E, K, M)) / np.sqrt(K)), "b": f32(0.5 * np.random.standard_normal((M, 1))), "offs": striped(two_experts())}


def reference(table, w, b, offs):
    idx = offs[:16].T.reshape(-1)
    x = f64(table)[:, idx]
    y = np.concatenate([f64(w)[e].T @ x[:, e * Q : (e + 1) * Q] for e in range(E)], axis=1)
    return gelu_tanh(y + f64(b))

@@ -1,0 +1,48 @@
+import concourse.mybir as mybir
+
+TOKENS, K, M, EXPERTS, PIECE = 1024, 512, 128, 4, 512
+P = 128
+BLOCKS = K // P
+OFFSET_COLUMNS = PIECE // 16
+FLOPS = 2 * K * M * EXPERTS * PIECE
+
+BF16, F32, U16 = mybir.dt.bfloat16, mybir.dt.float32, mybir.dt.uint16
+GELU_TANH = mybir.ActivationFunctionType.Gelu_apprx_tanh
+
+
+def tile_gather_matmul_kernel(tc, table, w, b, offs, out):
+    nc = tc.nc
+    table_view = table.rearrange("(p a) s -> p a s", a=BLOCKS)
+    w_view = w.rearrange("e (p a) m -> e p a m", a=BLOCKS)
+
+    with (
+        tc.tile_pool(name="held", bufs=1) as held,
+        tc.psum_pool(name="sums", bufs=1) as sums,
+    ):
+        weights = [held.tile([P, BLOCKS, M], BF16, name=f"weights{e}") for e in range(EXPERTS)]
+        blocks = [held.tile([P, TOKENS], BF16, name=f"block{a}") for a in range(BLOCKS)]
+        offsets = held.tile([P, EXPERTS * OFFSET_COLUMNS], U16, name="offsets")
+        bias = held.tile([P, 1], F32, name="bias")
+
+        nc.sync.dma_start(offsets[:], offs)
+        nc.sync.dma_start(weights[0][:], w_view[0])
+        for a in range(BLOCKS):
+            nc.sync.dma_start(blocks[a][:], table_view[:, a, :])
+        for e in range(1, EXPERTS):
+            nc.sync.dma_start(weights[e][:], w_view[e])
+        nc.scalar.dma_start(bias[:], b)
+
+        for e in range(EXPERTS):
+            piece = offsets[:, e * OFFSET_COLUMNS : (e + 1) * OFFSET_COLUMNS]
+            y = sums.tile([P, PIECE], F32, name=f"y{e}")
+            for a in range(BLOCKS):
+                nc.tensor.matmul(
+                    y[:],
+                    weights[e][:, a, :],
+                    blocks[a][:].indirect(piece),
+                    start=a == 0,
+                    stop=a == BLOCKS - 1,
+                )
+            activated = held.tile([P, PIECE], F32, name=f"activated{e}")
+            nc.scalar.activation(activated[:], y[:], GELU_TANH, bias=bias[:])
+            nc.sync.dma_start(out[:, e * PIECE : (e + 1) * PIECE], activated[:])

@@ -4,6 +4,7 @@ TOKENS, K, M, EXPERTS, PIECE = 1024, 512, 128, 4, 512
 P = 128
 BLOCKS = K // P
 OFFSET_COLUMNS = PIECE // 16
+HALF = PIECE // 2
 FLOPS = 2 * K * M * EXPERTS * PIECE
 
 BF16, F32, U16 = mybir.dt.bfloat16, mybir.dt.float32, mybir.dt.uint16
@@ -19,30 +20,40 @@ def tile_gather_matmul_kernel(tc, table, w, b, offs, out):
         tc.tile_pool(name="held", bufs=1) as held,
         tc.psum_pool(name="sums", bufs=1) as sums,
     ):
-        weights = [held.tile([P, BLOCKS, M], BF16, name=f"weights{e}") for e in range(EXPERTS)]
-        blocks = [held.tile([P, TOKENS], BF16, name=f"block{a}") for a in range(BLOCKS)]
         offsets = held.tile([P, EXPERTS * OFFSET_COLUMNS], U16, name="offsets")
+        blocks = [held.tile([P, TOKENS], BF16, name=f"block{a}") for a in range(BLOCKS)]
+        weights = [held.tile([P, BLOCKS, M], BF16, name=f"weights{e}") for e in range(EXPERTS)]
         bias = held.tile([P, 1], F32, name="bias")
 
         nc.sync.dma_start(offsets[:], offs)
-        nc.sync.dma_start(weights[0][:], w_view[0])
-        for a in range(BLOCKS):
-            nc.sync.dma_start(blocks[a][:], table_view[:, a, :])
-        for e in range(1, EXPERTS):
+        nc.sync.dma_start(blocks[0][:], table_view[:, 0, :])
+        for e in range(EXPERTS):
             nc.sync.dma_start(weights[e][:], w_view[e])
-        nc.scalar.dma_start(bias[:], b)
+        for a in range(1, BLOCKS):
+            nc.sync.dma_start(blocks[a][:], table_view[:, a, :])
+        nc.sync.dma_start(bias[:], b)
+
+        zero = held.tile([P, 1], F32, name="zero")
+        unread = held.tile([P, 1], F32, name="unread")
+        nc.vector.memset(zero[:], 0.0)
+        nc.scalar.activation(unread[:], zero[:], GELU_TANH)
+
+        y = [sums.tile([P, PIECE], F32, name=f"y{e}") for e in range(EXPERTS)]
+        rounds = [range(0, BLOCKS // 2), range(BLOCKS // 2, BLOCKS)]
+        for half in rounds:
+            for e in range(EXPERTS):
+                piece = offsets[:, e * OFFSET_COLUMNS : (e + 1) * OFFSET_COLUMNS]
+                for a in half:
+                    nc.tensor.matmul(
+                        y[e][:],
+                        weights[e][:, a, :],
+                        blocks[a][:].indirect(piece),
+                        start=a == 0,
+                        stop=a == BLOCKS - 1,
+                    )
 
         for e in range(EXPERTS):
-            piece = offsets[:, e * OFFSET_COLUMNS : (e + 1) * OFFSET_COLUMNS]
-            y = sums.tile([P, PIECE], F32, name=f"y{e}")
-            for a in range(BLOCKS):
-                nc.tensor.matmul(
-                    y[:],
-                    weights[e][:, a, :],
-                    blocks[a][:].indirect(piece),
-                    start=a == 0,
-                    stop=a == BLOCKS - 1,
-                )
-            activated = held.tile([P, PIECE], F32, name=f"activated{e}")
-            nc.scalar.activation(activated[:], y[:], GELU_TANH, bias=bias[:])
-            nc.sync.dma_start(out[:, e * PIECE : (e + 1) * PIECE], activated[:])
+            for first in range(0, PIECE, HALF):
+                activated = held.tile([P, HALF], F32, name=f"activated{e}_{first}")
+                nc.scalar.activation(activated[:], y[e][:, first : first + HALF], GELU_TANH, bias=bias[:])
+                nc.sync.dma_start(out[:, e * PIECE + first : e * PIECE + first + HALF], activated[:])

import concourse.mybir as mybir

TOKENS, K, M, EXPERTS, PIECE = 1024, 512, 128, 4, 512
P = 128
BLOCKS = K // P
OFFSET_COLUMNS = PIECE // 16
HALF = PIECE // 2
FLOPS = 2 * K * M * EXPERTS * PIECE

BF16, F32, U16 = mybir.dt.bfloat16, mybir.dt.float32, mybir.dt.uint16
GELU_TANH = mybir.ActivationFunctionType.Gelu_apprx_tanh


def tile_gather_matmul_kernel(tc, table, w, b, offs, out):
    nc = tc.nc
    table_view = table.rearrange("(p a) s -> p a s", a=BLOCKS)
    w_view = w.rearrange("e (p a) m -> e p a m", a=BLOCKS)

    with (
        tc.tile_pool(name="held", bufs=1) as held,
        tc.psum_pool(name="sums", bufs=1) as sums,
    ):
        offsets = held.tile([P, EXPERTS * OFFSET_COLUMNS], U16, name="offsets")
        blocks = [held.tile([P, TOKENS], BF16, name=f"block{a}") for a in range(BLOCKS)]
        weights = [held.tile([P, BLOCKS, M], BF16, name=f"weights{e}") for e in range(EXPERTS)]
        bias = held.tile([P, 1], F32, name="bias")

        nc.sync.dma_start(offsets[:], offs)
        nc.sync.dma_start(blocks[0][:], table_view[:, 0, :])
        for e in range(EXPERTS):
            nc.sync.dma_start(weights[e][:], w_view[e])
        for a in range(1, BLOCKS):
            nc.sync.dma_start(blocks[a][:], table_view[:, a, :])
        nc.sync.dma_start(bias[:], b)

        zero = held.tile([P, 1], F32, name="zero")
        unread = held.tile([P, 1], F32, name="unread")
        nc.vector.memset(zero[:], 0.0)
        nc.scalar.activation(unread[:], zero[:], GELU_TANH)

        y = [sums.tile([P, PIECE], F32, name=f"y{e}") for e in range(EXPERTS)]
        rounds = [range(0, BLOCKS // 2), range(BLOCKS // 2, BLOCKS)]
        for half in rounds:
            for e in range(EXPERTS):
                piece = offsets[:, e * OFFSET_COLUMNS : (e + 1) * OFFSET_COLUMNS]
                for a in half:
                    nc.tensor.matmul(
                        y[e][:],
                        weights[e][:, a, :],
                        blocks[a][:].indirect(piece),
                        start=a == 0,
                        stop=a == BLOCKS - 1,
                    )

        for e in range(EXPERTS):
            for first in range(0, PIECE, HALF):
                activated = held.tile([P, HALF], F32, name=f"activated{e}_{first}")
                nc.scalar.activation(activated[:], y[e][:, first : first + HALF], GELU_TANH, bias=bias[:])
                nc.sync.dma_start(out[:, e * PIECE + first : e * PIECE + first + HALF], activated[:])
